import numpy as np
import ml_dtypes


def mxq(x, axis, fmt="e4m3"):
    dtype, down = {"e4m3": (ml_dtypes.float8_e4m3fn, 7), "e5m2": (ml_dtypes.float8_e5m2, 14)}[fmt]
    v = np.moveaxis(np.asarray(x, np.float32).astype(ml_dtypes.bfloat16).astype(np.float64), axis, -1)
    blocks = v.reshape(v.shape[:-1] + (-1, 32))
    amax = np.abs(blocks).max(-1, keepdims=True)
    byte = np.maximum(np.where(amax > 0, np.frexp(amax)[1] - 1 + 127, 0) - down, 1)
    scale = np.exp2(byte - 127.0)
    codes = (blocks / scale).astype(np.float32).astype(dtype).astype(np.float64)
    return np.moveaxis((codes * scale).reshape(v.shape), -1, axis)


WIDE = False


def mx_kscale(k):
    if not WIDE:
        return np.ones(k)
    levels = np.array([30, -30])
    if k % 512:
        return np.exp2(np.random.permutation(np.resize(levels, k // 32))).repeat(32)
    a = np.empty((k // 512, 16))
    for p in range(k // 512):
        a[p, :8] = np.random.permutation(np.resize(levels, 8))
        for g in range(8):
            far = levels[np.abs(levels - a[p, g]) >= 10]
            a[p, g + 8] = far[np.random.randint(len(far))]
    return np.exp2(a.ravel()).repeat(32)


def f64(x):
    return np.asarray(x).astype(np.float64)


def striped(idx):
    return np.tile(np.asarray(idx).reshape(-1, 16).T, (8, 1)).astype(np.uint16)


def unstriped(offs):
    return offs[:16].T.reshape(-1).astype(np.int64)


def striped8(idx):
    return np.asarray(idx).reshape(8, -1, 16).transpose(0, 2, 1).reshape(128, -1).astype(np.uint16)


def unstriped8(offs):
    return offs.reshape(8, 16, -1).transpose(0, 2, 1).reshape(8, -1).astype(np.int64)


def pick8(x, idx, run):
    r = np.arange(len(x))
    return x[r[:, None], idx[r % (8 * run) // run]]


E2M1 = np.array([0.0, 0.5, 1.0, 1.5, 2.0, 3.0, 4.0, 6.0, -0.0, -0.5, -1.0, -1.5, -2.0, -3.0, -4.0, -6.0])


def pack_weight(w, fmt):
    k, n = w.shape
    w = f64(np.asarray(w, np.float32).astype(ml_dtypes.bfloat16)).reshape(k // 32, 32, n)
    amax = np.abs(w).max(1)
    if fmt in ("e4m3", "e5m2"):
        byte = np.frexp(amax)[1] - 1 + 127 - (7 if fmt == "e4m3" else 14)
    else:
        mant, ex = np.frexp(amax / 6.0)
        byte = np.where(mant > 0.5, ex, ex - 1) + 127
    byte = np.clip(np.where(amax > 0, byte, 1), 1, 254)
    scaled = (w * np.exp2(127.0 - byte)[:, None, :]).reshape(k, n).astype(np.float32)
    by_word = np.ascontiguousarray(scaled.reshape(k // 512, 128, 4, n).transpose(0, 1, 3, 2))
    if fmt in ("e4m3", "e5m2"):
        words = by_word.astype(ml_dtypes.float8_e4m3fn if fmt == "e4m3" else ml_dtypes.float8_e5m2).view(np.uint8)
    else:
        c = by_word.astype(ml_dtypes.float4_e2m1fn).view(np.uint8) & 0xF
        words = (c[..., 0::2] | (c[..., 1::2] << 4)).reshape(k // 512, 128, 2 * n)
    return np.ascontiguousarray(words), np.ascontiguousarray(byte.astype(np.uint8).reshape(k // 512, 16, n))


def unpack_weight(words, scales, fmt):
    g, _, n = scales.shape
    words = np.ascontiguousarray(words).reshape(g, 128, n, -1)
    if fmt in ("e4m3", "e5m2"):
        vals = words.view(ml_dtypes.float8_e4m3fn if fmt == "e4m3" else ml_dtypes.float8_e5m2).astype(np.float64)
    else:
        nib = np.empty((g, 128, n, 4), np.uint8)
        nib[..., 0::2] = words & 0xF
        nib[..., 1::2] = words >> 4
        vals = E2M1[nib]
    vals = vals * np.repeat(np.exp2(scales.astype(np.float64) - 127.0), 8, axis=1)[..., None]
    return vals.transpose(0, 1, 3, 2).reshape(g * 512, n)


K, T, J, R, F, Z, N = 512, 512, 256, 512, 512, 1024, 256


def setup_inputs():
    n = np.random.standard_normal
    idx = np.stack([np.random.permutation(T)[:J] for _ in range(8)])
    idx2 = np.random.permutation(Z)[:J]
    fk = mx_kscale(K)
    fr = mx_kscale(R)
    ff = mx_kscale(F)
    xtp = pack_weight(n((K, T)) / fk[:, None], "e5m2")
    wp = pack_weight(n((K, R)) * 1 / np.sqrt(K) * fk[:, None] * fr, "e2m1")
    w2p = pack_weight(n((F, R)) * 1 / np.sqrt(F) * ff[:, None] * fr, "e2m1")
    wbp = pack_weight(n((R, N)) * 1 / np.sqrt(R) / fr[:, None], "e4m3")
    return {
        "xt_words": xtp[0],
        "xt_scales": xtp[1],
        "w_words": wp[0],
        "w_scales": wp[1],
        "xo": (n((F, Z))).astype(np.float32),
        "fl": (np.random.uniform(0.5, 2.0, (F, 1)) / ff[:, None]).astype(np.float32),
        "so": (n((F, J)) * 0.8).astype(np.float32),
        "w2_words": w2p[0],
        "w2_scales": w2p[1],
        "wb_words": wbp[0],
        "wb_scales": wbp[1],
        "rs": (n((N, J))).astype(np.float32),
        "gm": (np.random.uniform(0.5, 2.0, (N, 1))).astype(np.float32),
        "offs": striped8(idx),
        "offs2": striped(idx2),
    }


def reference(xt_words, xt_scales, w_words, w_scales, xo, fl, so, w2_words, w2_scales, wb_words, wb_scales, rs, gm, offs, offs2):
    idx = unstriped8(offs)
    idx2 = unstriped(offs2)
    xtu = unpack_weight(xt_words, xt_scales, "e5m2")
    wu = unpack_weight(w_words, w_scales, "e2m1")
    w2u = unpack_weight(w2_words, w2_scales, "e2m1")
    wbu = unpack_weight(wb_words, wb_scales, "e4m3")
    u2 = np.maximum(f64(xo)[:, idx2], f64(so)) * f64(fl)
    xtidxg = pick8(xtu, idx, 64)
    a = wu.T @ xtidxg
    u2q = mxq(u2, 0, "e4m3")
    q = w2u.T @ u2q
    y1 = np.pad(q, ((0, 0), (1, 0)))[:, :J]
    hid = np.maximum(a, q - 0.6 * y1)
    hidq = mxq(hid, 0, "e5m2")
    p = wbu.T @ hidq
    y = f64(gm) * p + f64(rs)
    return y

@@ -1,0 +1,204 @@
+import concourse.mybir as mybir
+
+K, T, J, R, F, Z, N = 512, 512, 256, 512, 512, 1024, 256
+FLOPS = 2 * J * (K * R + F * R + R * N)
+
+F32 = mybir.dt.float32
+BF16 = mybir.dt.bfloat16
+I32 = mybir.dt.int32
+U32 = mybir.dt.uint32
+U16 = mybir.dt.uint16
+U8 = mybir.dt.uint8
+E4M3 = mybir.dt.float8_e4m3fn_x4
+E5M2 = mybir.dt.float8_e5m2_x4
+E2M1 = mybir.dt.float4_e2m1fn_x4
+ALU = mybir.AluOpType
+COPY = mybir.ActivationFunctionType.Copy
+
+P = 128
+PACK = 4
+HALF = J // 2
+QUARTER = J // 4
+W_COL, W2_COL, WB_COL, XT_COL = 0, R, 2 * R, 2 * R + N
+SCALE_COLS = XT_COL + J
+
+
+def tile_list_two_headpicks_largest_stepgap_residual_kernel(
+    tc, xt_words, xt_scales, w_words, w_scales, xo, fl, so, w2_words, w2_scales,
+    wb_words, wb_scales, rs, gm, offs, offs2, out,
+):
+    nc = tc.nc
+    with (
+        tc.tile_pool(name="sbuf", bufs=1) as sb,
+        tc.psum_pool(name="psum", bufs=1) as ps,
+    ):
+        offs_sb = sb.tile([P, J // 16], U16)
+        offs2_sb = sb.tile([P, J // 16], U16)
+        xt_scale_raw = sb.tile([P, T], U8, align_bytes=64)
+        w_scale_raw = sb.tile([P, 2 * R], U8, align_bytes=64)
+        scales = sb.tile([P, SCALE_COLS], U8, align_bytes=64)
+        w_raw = sb.tile([P, 2 * R], U8, align_bytes=64)
+        w2_raw = sb.tile([P, 2 * R], U8, align_bytes=64)
+        xt_sb = sb.tile([P, T], U32, align_bytes=64)
+        xo_first = sb.tile([P, 2, Z], F32)
+        xo_third = sb.tile([P, Z], F32)
+        xo_last = sb.tile([P, Z], F32)
+        so_first = sb.tile([P, 3, J], F32)
+        so_last = sb.tile([P, J], F32)
+        fl_sb = sb.tile([P, PACK], F32)
+        gm_sb = sb.tile([P, 2], F32)
+        wb_sb = sb.tile([P, N], U32, align_bytes=64)
+        rs_sb = sb.tile([P, 2, J], F32)
+        q_sb = sb.tile([P, J + 1, PACK], F32)
+
+        nc.gpsimd.memset(xt_scale_raw[:].bitcast(I32), 0)
+        nc.vector.memset(w_scale_raw[:].bitcast(I32), 0)
+        nc.vector.memset(scales[:, WB_COL:XT_COL].bitcast(I32), 0)
+        nc.vector.memset(q_sb[:, 0, :], 0.0)
+
+        xo_planes = xo.rearrange("(p t) z -> p t z", t=PACK)
+        so_planes = so.rearrange("(p t) j -> p t j", t=PACK)
+        nc.sync.dma_start(offs_sb[:], offs)
+        nc.sync.dma_start(xt_scale_raw[0:P:8, :].bitcast(I32), xt_scales[0].bitcast(I32))
+        nc.sync.dma_start(w_scale_raw[0:P:8, R:].bitcast(I32), w2_scales[0].bitcast(I32))
+        nc.sync.dma_start(w_scale_raw[0:P:8, :R].bitcast(I32), w_scales[0].bitcast(I32))
+        nc.sync.dma_start(scales[0:P:8, WB_COL:XT_COL].bitcast(I32), wb_scales[0].bitcast(I32))
+        nc.sync.dma_start(w2_raw[:].bitcast(I32), w2_words[0].bitcast(I32))
+        nc.sync.dma_start(w_raw[:].bitcast(I32), w_words[0].bitcast(I32))
+        nc.sync.dma_start(xo_first[:], xo_planes[:, 0:2, :])
+        nc.sync.dma_start(offs2_sb[:], offs2)
+        nc.sync.dma_start(fl_sb[:], fl.rearrange("(p t) o -> p (t o)", t=PACK))
+        nc.sync.dma_start(so_first[:], so_planes[:, 0:3, :])
+        nc.sync.dma_start(xo_third[:], xo_planes[:, 2, :])
+        nc.sync.dma_start(xo_last[:], xo_planes[:, 3, :])
+        nc.sync.dma_start(so_last[:], so_planes[:, 3, :])
+        nc.sync.dma_start(
+            xt_sb[:].bitcast(I32), xt_words[0].rearrange("p n t -> p (n t)").bitcast(I32)
+        )
+
+        xt_scale_picked = sb.tile([P, J], U8, align_bytes=64)
+        nc.vector.tensor_copy(xt_scale_picked[:], xt_scale_raw[:].indirect(offs_sb[:]))
+        nc.vector.tensor_copy(
+            scales[:, W_COL:WB_COL].rearrange("p (w t m) -> p w t m", w=2, t=PACK),
+            w_scale_raw[:].rearrange("p (w m t) -> p w t m", w=2, t=PACK),
+        )
+        nc.vector.tensor_copy(scales[:, XT_COL:].bitcast(I32), xt_scale_picked[:].bitcast(I32))
+        for r in range(1, 4):
+            nc.sync.dma_start(scales[r:P:32, :].bitcast(I32), scales[8 * r:P:32, :].bitcast(I32))
+
+        nc.sync.dma_start(
+            wb_sb[:].bitcast(I32), wb_words[0].rearrange("p n t -> p (n t)").bitcast(I32)
+        )
+        nc.sync.dma_start(rs_sb[:], rs.rearrange("(c p) j -> p c j", p=P))
+        with nc.allow_non_contiguous_dma(reason="one factor a partition and output slice"):
+            nc.sync.dma_start(gm_sb[:], gm.rearrange("(c p) o -> p (c o)", p=P))
+
+        w_dealt = sb.tile([P, 2 * R], U8, align_bytes=64)
+        w2_dealt = sb.tile([P, 2 * R], U8, align_bytes=64)
+        for dealt, raw in ((w2_dealt, w2_raw), (w_dealt, w_raw)):
+            nc.vector.tensor_copy(
+                dealt[:].bitcast(U16).rearrange("p (t m) -> p t m", t=PACK),
+                raw[:].bitcast(U16).rearrange("p (m t) -> p t m", t=PACK),
+            )
+
+        def hidden_product(bank, dealt, w_col, codes, code_dtype, plane, h):
+            for t in range(PACK):
+                nc.tensor.matmul_mx(
+                    out=bank[:, t, :],
+                    lhsT=dealt[:, 2 * P * t:2 * P * (t + 1)].bitcast(E2M1),
+                    lhsT_scale=scales[:, w_col + P * t:w_col + P * (t + 1)],
+                    rhs=codes[:, h * HALF:(h + 1) * HALF].bitcast(code_dtype),
+                    rhs_scale=plane[:, h * HALF:(h + 1) * HALF],
+                    start=True,
+                    stop=True,
+                )
+
+        picked = sb.tile([P, 3, J], F32)
+        picked_last = [sb.tile([P, HALF], F32, name="picked_last%d" % h) for h in range(2)]
+        larger = sb.tile([P, PACK, J], F32)
+        u2 = sb.tile([P, J, PACK], BF16, align_bytes=64)
+        windows = [xo_first[:, 0, :], xo_first[:, 1, :], xo_third[:]]
+        for t in range(3):
+            nc.scalar.activation(picked[:, t, :], windows[t].indirect(offs2_sb[:]), COPY)
+            nc.vector.tensor_tensor(larger[:, t, :], picked[:, t, :], so_first[:, t, :], ALU.max)
+            nc.vector.tensor_scalar(
+                u2[:, :, t], larger[:, t, :], fl_sb[:, t:t + 1], None, ALU.mult
+            )
+        nc.vector.tensor_copy(picked_last[0][:], xo_last[:].indirect(offs2_sb[:, 0:8]))
+        nc.scalar.activation(picked_last[1][:], xo_last[:].indirect(offs2_sb[:, 8:16]), COPY)
+        halves = [slice(h * HALF, (h + 1) * HALF) for h in range(2)]
+        for h in range(2):
+            nc.vector.tensor_tensor(
+                larger[:, 3, halves[h]], picked_last[h][:], so_last[:, halves[h]], ALU.max
+            )
+        for h in range(2):
+            nc.vector.tensor_scalar(
+                u2[:, halves[h], 3], larger[:, 3, halves[h]], fl_sb[:, 3:4], None, ALU.mult
+            )
+        u2_codes = sb.tile([P, J], U32, align_bytes=64)
+        u2_scales = sb.tile([P, J], U8, align_bytes=64)
+        q_ps = [ps.tile([P, PACK, HALF], F32, name="q_ps%d" % h) for h in range(2)]
+        for h in range(2):
+            nc.vector.quantize_mx(
+                out=u2_codes[:, halves[h]].bitcast(E4M3),
+                scales=u2_scales[:, halves[h]],
+                in_=u2[:, halves[h], :].rearrange("p j t -> p (j t)"),
+            )
+            hidden_product(q_ps[h], w2_dealt, W2_COL, u2_codes, E4M3, u2_scales, h)
+
+        xt_picked = sb.tile([P, J], U32, align_bytes=64)
+        nc.vector.tensor_copy(xt_picked[:], xt_sb[:].indirect(offs_sb[:]))
+        a_ps = [ps.tile([P, PACK, HALF], F32, name="a_ps%d" % h) for h in range(2)]
+        for h in range(2):
+            hidden_product(a_ps[h], w_dealt, W_COL, xt_picked, E5M2, scales[:, XT_COL:], h)
+
+        step = sb.tile([P, J, PACK], F32)
+        for c in range(4):
+            j0 = c * QUARTER
+            in_bank = j0 % HALF
+            nc.scalar.activation(
+                q_sb[:, 1 + j0:1 + j0 + QUARTER, :],
+                q_ps[c // 2][:, :, in_bank:in_bank + QUARTER].rearrange("p t j -> p j t"),
+                COPY,
+            )
+            nc.vector.scalar_tensor_tensor(
+                step[:, j0:j0 + QUARTER, :],
+                q_sb[:, j0:j0 + QUARTER, :],
+                -0.6,
+                q_sb[:, 1 + j0:1 + j0 + QUARTER, :],
+                ALU.mult,
+                ALU.add,
+            )
+        hid = sb.tile([P, J, PACK], BF16, align_bytes=64)
+        for h in range(2):
+            nc.vector.tensor_tensor(
+                hid[:, halves[h], :],
+                step[:, halves[h], :],
+                a_ps[h][:].rearrange("p t j -> p j t"),
+                ALU.max,
+            )
+        hid_codes = sb.tile([P, J], U32, align_bytes=64)
+        hid_scales = sb.tile([P, J], U8, align_bytes=64)
+        p_ps = [ps.tile([P, J], F32, name="p_ps%d" % c) for c in range(2)]
+        for h in range(2):
+            nc.vector.quantize_mx(
+                out=hid_codes[:, halves[h]].bitcast(E5M2),
+                scales=hid_scales[:, halves[h]],
+                in_=hid[:, halves[h], :].rearrange("p j t -> p (j t)"),
+            )
+            for c in range(2):
+                nc.tensor.matmul_mx(
+                    out=p_ps[c][:, halves[h]],
+                    lhsT=wb_sb[:, P * c:P * (c + 1)].bitcast(E4M3),
+                    lhsT_scale=scales[:, WB_COL + P * c:WB_COL + P * (c + 1)],
+                    rhs=hid_codes[:, halves[h]].bitcast(E5M2),
+                    rhs_scale=hid_scales[:, halves[h]],
+                    start=True,
+                    stop=True,
+                )
+        for c, queue in ((0, nc.sync), (1, nc.scalar)):
+            result = sb.tile([P, J], F32, name="result%d" % c)
+            nc.vector.scalar_tensor_tensor(
+                result[:], p_ps[c][:], gm_sb[:, c:c + 1], rs_sb[:, c, :], ALU.mult, ALU.add
+            )
+            queue.dma_start(out[P * c:P * (c + 1), :], result[:])

@@ -40,10 +40,9 @@ def tile_list_two_headpicks_largest_stepgap_residual_kernel(
         w_raw = sb.tile([P, 2 * R], U8, align_bytes=64)
         w2_raw = sb.tile([P, 2 * R], U8, align_bytes=64)
         xt_sb = sb.tile([P, T], U32, align_bytes=64)
-        xo_first = sb.tile([P, 2, Z], F32)
-        xo_third = sb.tile([P, Z], F32)
-        xo_last = sb.tile([P, Z], F32)
-        so_first = sb.tile([P, 3, J], F32)
+        xo_sb = [sb.tile([P, Z], F32, name="xo_sb%d" % t) for t in range(PACK)]
+        so_first = sb.tile([P, 2, J], F32)
+        so_third = sb.tile([P, J], F32)
         so_last = sb.tile([P, J], F32)
         fl_sb = sb.tile([P, PACK], F32)
         gm_sb = sb.tile([P, 2], F32)
@@ -51,30 +50,35 @@ def tile_list_two_headpicks_largest_stepgap_residual_kernel(
         rs_sb = sb.tile([P, 2, J], F32)
         q_sb = sb.tile([P, J + 1, PACK], F32)
 
-        nc.gpsimd.memset(xt_scale_raw[:].bitcast(I32), 0)
-        nc.vector.memset(w_scale_raw[:].bitcast(I32), 0)
+        zero = sb.tile([P, PACK], F32)
+        nc.vector.memset(xt_scale_raw[:].bitcast(I32), 0)
+        nc.vector.memset(w_scale_raw[:, R:].bitcast(I32), 0)
+        nc.gpsimd.memset(w_scale_raw[:, :R].bitcast(I32), 0)
         nc.vector.memset(scales[:, WB_COL:XT_COL].bitcast(I32), 0)
-        nc.vector.memset(q_sb[:, 0, :], 0.0)
+        nc.gpsimd.memset(zero[:], 0.0)
+        nc.scalar.activation(q_sb[:, 0, :], zero[:], COPY)
 
         xo_planes = xo.rearrange("(p t) z -> p t z", t=PACK)
         so_planes = so.rearrange("(p t) j -> p t j", t=PACK)
         nc.sync.dma_start(offs_sb[:], offs)
+        nc.sync.dma_start(offs2_sb[:], offs2)
+        nc.sync.dma_start(xo_sb[0][:], xo_planes[:, 0, :])
+        nc.sync.dma_start(w2_raw[:].bitcast(I32), w2_words[0].bitcast(I32))
         nc.sync.dma_start(xt_scale_raw[0:P:8, :].bitcast(I32), xt_scales[0].bitcast(I32))
         nc.sync.dma_start(w_scale_raw[0:P:8, R:].bitcast(I32), w2_scales[0].bitcast(I32))
         nc.sync.dma_start(w_scale_raw[0:P:8, :R].bitcast(I32), w_scales[0].bitcast(I32))
-        nc.sync.dma_start(scales[0:P:8, WB_COL:XT_COL].bitcast(I32), wb_scales[0].bitcast(I32))
-        nc.sync.dma_start(w2_raw[:].bitcast(I32), w2_words[0].bitcast(I32))
-        nc.sync.dma_start(w_raw[:].bitcast(I32), w_words[0].bitcast(I32))
-        nc.sync.dma_start(xo_first[:], xo_planes[:, 0:2, :])
-        nc.sync.dma_start(offs2_sb[:], offs2)
+        nc.sync.dma_start(xo_sb[1][:], xo_planes[:, 1, :])
+        nc.sync.dma_start(so_first[:], so_planes[:, 0:2, :])
         nc.sync.dma_start(fl_sb[:], fl.rearrange("(p t) o -> p (t o)", t=PACK))
-        nc.sync.dma_start(so_first[:], so_planes[:, 0:3, :])
-        nc.sync.dma_start(xo_third[:], xo_planes[:, 2, :])
-        nc.sync.dma_start(xo_last[:], xo_planes[:, 3, :])
+        nc.sync.dma_start(xo_sb[2][:], xo_planes[:, 2, :])
+        nc.sync.dma_start(so_third[:], so_planes[:, 2, :])
+        nc.sync.dma_start(scales[0:P:8, WB_COL:XT_COL].bitcast(I32), wb_scales[0].bitcast(I32))
+        nc.sync.dma_start(xo_sb[3][:], xo_planes[:, 3, :])
         nc.sync.dma_start(so_last[:], so_planes[:, 3, :])
         nc.sync.dma_start(
             xt_sb[:].bitcast(I32), xt_words[0].rearrange("p n t -> p (n t)").bitcast(I32)
         )
+        nc.sync.dma_start(w_raw[:].bitcast(I32), w_words[0].bitcast(I32))
 
         xt_scale_picked = sb.tile([P, J], U8, align_bytes=64)
         nc.vector.tensor_copy(xt_scale_picked[:], xt_scale_raw[:].indirect(offs_sb[:]))
@@ -93,13 +97,14 @@ def tile_list_two_headpicks_largest_stepgap_residual_kernel(
         with nc.allow_non_contiguous_dma(reason="one factor a partition and output slice"):
             nc.sync.dma_start(gm_sb[:], gm.rearrange("(c p) o -> p (c o)", p=P))
 
-        w_dealt = sb.tile([P, 2 * R], U8, align_bytes=64)
-        w2_dealt = sb.tile([P, 2 * R], U8, align_bytes=64)
-        for dealt, raw in ((w2_dealt, w2_raw), (w_dealt, w_raw)):
+        def deal_words(dealt, raw):
             nc.vector.tensor_copy(
                 dealt[:].bitcast(U16).rearrange("p (t m) -> p t m", t=PACK),
                 raw[:].bitcast(U16).rearrange("p (m t) -> p t m", t=PACK),
             )
+
+        w2_dealt = sb.tile([P, 2 * R], U8, align_bytes=64)
+        deal_words(w2_dealt, w2_raw)
 
         def hidden_product(bank, dealt, w_col, codes, code_dtype, plane, h):
             for t in range(PACK):
@@ -115,17 +120,22 @@ def tile_list_two_headpicks_largest_stepgap_residual_kernel(
 
         picked = sb.tile([P, 3, J], F32)
         picked_last = [sb.tile([P, HALF], F32, name="picked_last%d" % h) for h in range(2)]
-        larger = sb.tile([P, PACK, J], F32)
-        u2 = sb.tile([P, J, PACK], BF16, align_bytes=64)
-        windows = [xo_first[:, 0, :], xo_first[:, 1, :], xo_third[:]]
-        for t in range(3):
-            nc.scalar.activation(picked[:, t, :], windows[t].indirect(offs2_sb[:]), COPY)
-            nc.vector.tensor_tensor(larger[:, t, :], picked[:, t, :], so_first[:, t, :], ALU.max)
-            nc.vector.tensor_scalar(
-                u2[:, :, t], larger[:, t, :], fl_sb[:, t:t + 1], None, ALU.mult
+        larger = sb.tile([P, PACK, J], F32, align_bytes=64, tag="larger_then_w")
+        u2 = sb.tile([P, J, PACK], BF16, align_bytes=64, tag="u2_then_xt")
+        u2_pair = sb.tile([P, 2, J], BF16)
+        for t in range(2):
+            nc.scalar.activation(picked[:, t, :], xo_sb[t][:].indirect(offs2_sb[:]), COPY)
+        nc.vector.tensor_tensor(larger[:, 0:2, :], picked[:, 0:2, :], so_first[:], ALU.max)
+        for t in range(2):
+            nc.scalar.activation(u2_pair[:, t, :], larger[:, t, :], COPY, scale=fl_sb[:, t:t + 1])
+        nc.vector.tensor_copy(u2[:, :, 0:2], u2_pair[:].rearrange("p t j -> p j t"))
+        nc.scalar.activation(picked[:, 2, :], xo_sb[2][:].indirect(offs2_sb[:]), COPY)
+        nc.vector.tensor_tensor(larger[:, 2, :], picked[:, 2, :], so_third[:], ALU.max)
+        nc.vector.tensor_scalar(u2[:, :, 2], larger[:, 2, :], fl_sb[:, 2:3], None, ALU.mult)
+        for h in range(2):
+            nc.scalar.activation(
+                picked_last[h][:], xo_sb[3][:].indirect(offs2_sb[:, 8 * h:8 * (h + 1)]), COPY
             )
-        nc.vector.tensor_copy(picked_last[0][:], xo_last[:].indirect(offs2_sb[:, 0:8]))
-        nc.scalar.activation(picked_last[1][:], xo_last[:].indirect(offs2_sb[:, 8:16]), COPY)
         halves = [slice(h * HALF, (h + 1) * HALF) for h in range(2)]
         for h in range(2):
             nc.vector.tensor_tensor(
@@ -146,7 +156,9 @@ def tile_list_two_headpicks_largest_stepgap_residual_kernel(
             )
             hidden_product(q_ps[h], w2_dealt, W2_COL, u2_codes, E4M3, u2_scales, h)
 
-        xt_picked = sb.tile([P, J], U32, align_bytes=64)
+        w_dealt = sb.tile([P, 2 * R], U8, align_bytes=64, tag="larger_then_w")
+        deal_words(w_dealt, w_raw)
+        xt_picked = sb.tile([P, J], U32, align_bytes=64, tag="u2_then_xt")
         nc.vector.tensor_copy(xt_picked[:], xt_sb[:].indirect(offs_sb[:]))
         a_ps = [ps.tile([P, PACK, HALF], F32, name="a_ps%d" % h) for h in range(2)]
         for h in range(2):
@@ -179,7 +191,10 @@ def tile_list_two_headpicks_largest_stepgap_residual_kernel(
             )
         hid_codes = sb.tile([P, J], U32, align_bytes=64)
         hid_scales = sb.tile([P, J], U8, align_bytes=64)
-        p_ps = [ps.tile([P, J], F32, name="p_ps%d" % c) for c in range(2)]
+        out_rows = out.rearrange("(c p) j -> p c j", p=P)
+        p_ps = [
+            [ps.tile([P, HALF], F32, name="p_ps%d%d" % (h, c)) for c in range(2)] for h in range(2)
+        ]
         for h in range(2):
             nc.vector.quantize_mx(
                 out=hid_codes[:, halves[h]].bitcast(E5M2),
@@ -188,7 +203,7 @@ def tile_list_two_headpicks_largest_stepgap_residual_kernel(
             )
             for c in range(2):
                 nc.tensor.matmul_mx(
-                    out=p_ps[c][:, halves[h]],
+                    out=p_ps[h][c][:],
                     lhsT=wb_sb[:, P * c:P * (c + 1)].bitcast(E4M3),
                     lhsT_scale=scales[:, WB_COL + P * c:WB_COL + P * (c + 1)],
                     rhs=hid_codes[:, halves[h]].bitcast(E5M2),
@@ -196,9 +211,11 @@ def tile_list_two_headpicks_largest_stepgap_residual_kernel(
                     start=True,
                     stop=True,
                 )
-        for c, queue in ((0, nc.sync), (1, nc.scalar)):
-            result = sb.tile([P, J], F32, name="result%d" % c)
-            nc.vector.scalar_tensor_tensor(
-                result[:], p_ps[c][:], gm_sb[:, c:c + 1], rs_sb[:, c, :], ALU.mult, ALU.add
-            )
-            queue.dma_start(out[P * c:P * (c + 1), :], result[:])
+        for h, queue in ((0, nc.sync), (1, nc.scalar)):
+            result = sb.tile([P, 2, HALF], F32, name="result%d" % h)
+            for c in range(2):
+                nc.vector.scalar_tensor_tensor(
+                    result[:, c, :], p_ps[h][c][:], gm_sb[:, c:c + 1], rs_sb[:, c, halves[h]],
+                    ALU.mult, ALU.add,
+                )
+            queue.dma_start(out_rows[:, :, halves[h]], result[:])

@@ -19,7 +19,7 @@ P = 128
 PACK = 4
 HALF = J // 2
 QUARTER = J // 4
-W_COL, W2_COL, WB_COL, XT_COL = 0, R, 2 * R, 2 * R + N
+W_COL, W2_COL, XT_COL = 0, R, 2 * R
 SCALE_COLS = XT_COL + J
 
 
@@ -37,6 +37,7 @@ def tile_list_two_headpicks_largest_stepgap_residual_kernel(
         xt_scale_raw = sb.tile([P, T], U8, align_bytes=64)
         w_scale_raw = sb.tile([P, 2 * R], U8, align_bytes=64)
         scales = sb.tile([P, SCALE_COLS], U8, align_bytes=64)
+        wb_plane = sb.tile([P, N], U8, align_bytes=64)
         w_raw = sb.tile([P, 2 * R], U8, align_bytes=64)
         w2_raw = sb.tile([P, 2 * R], U8, align_bytes=64)
         xt_sb = sb.tile([P, T], U32, align_bytes=64)
@@ -54,8 +55,8 @@ def tile_list_two_headpicks_largest_stepgap_residual_kernel(
         nc.vector.memset(xt_scale_raw[:].bitcast(I32), 0)
         nc.vector.memset(w_scale_raw[:, R:].bitcast(I32), 0)
         nc.gpsimd.memset(w_scale_raw[:, :R].bitcast(I32), 0)
-        nc.vector.memset(scales[:, WB_COL:XT_COL].bitcast(I32), 0)
         nc.gpsimd.memset(zero[:], 0.0)
+        nc.gpsimd.memset(wb_plane[:].bitcast(I32), 0)
         nc.scalar.activation(q_sb[:, 0, :], zero[:], COPY)
 
         xo_planes = xo.rearrange("(p t) z -> p t z", t=PACK)
@@ -67,12 +68,11 @@ def tile_list_two_headpicks_largest_stepgap_residual_kernel(
         nc.sync.dma_start(xt_scale_raw[0:P:8, :].bitcast(I32), xt_scales[0].bitcast(I32))
         nc.sync.dma_start(w_scale_raw[0:P:8, R:].bitcast(I32), w2_scales[0].bitcast(I32))
         nc.sync.dma_start(w_scale_raw[0:P:8, :R].bitcast(I32), w_scales[0].bitcast(I32))
-        nc.sync.dma_start(xo_sb[1][:], xo_planes[:, 1, :])
         nc.sync.dma_start(so_first[:], so_planes[:, 0:2, :])
-        nc.sync.dma_start(fl_sb[:], fl.rearrange("(p t) o -> p (t o)", t=PACK))
+        nc.gpsimd.dma_start(fl_sb[:], fl.rearrange("(p t) o -> p (t o)", t=PACK))
+        nc.sync.dma_start(xo_sb[1][:], xo_planes[:, 1, :])
         nc.sync.dma_start(xo_sb[2][:], xo_planes[:, 2, :])
         nc.sync.dma_start(so_third[:], so_planes[:, 2, :])
-        nc.sync.dma_start(scales[0:P:8, WB_COL:XT_COL].bitcast(I32), wb_scales[0].bitcast(I32))
         nc.sync.dma_start(xo_sb[3][:], xo_planes[:, 3, :])
         nc.sync.dma_start(so_last[:], so_planes[:, 3, :])
         nc.sync.dma_start(
@@ -83,7 +83,7 @@ def tile_list_two_headpicks_largest_stepgap_residual_kernel(
         xt_scale_picked = sb.tile([P, J], U8, align_bytes=64)
         nc.vector.tensor_copy(xt_scale_picked[:], xt_scale_raw[:].indirect(offs_sb[:]))
         nc.vector.tensor_copy(
-            scales[:, W_COL:WB_COL].rearrange("p (w t m) -> p w t m", w=2, t=PACK),
+            scales[:, W_COL:XT_COL].rearrange("p (w t m) -> p w t m", w=2, t=PACK),
             w_scale_raw[:].rearrange("p (w m t) -> p w t m", w=2, t=PACK),
         )
         nc.vector.tensor_copy(scales[:, XT_COL:].bitcast(I32), xt_scale_picked[:].bitcast(I32))
@@ -93,6 +93,8 @@ def tile_list_two_headpicks_largest_stepgap_residual_kernel(
         nc.sync.dma_start(
             wb_sb[:].bitcast(I32), wb_words[0].rearrange("p n t -> p (n t)").bitcast(I32)
         )
+        for r in range(4):
+            nc.sync.dma_start(wb_plane[r:P:32, :].bitcast(I32), wb_scales[0, r:16:4, :].bitcast(I32))
         nc.sync.dma_start(rs_sb[:], rs.rearrange("(c p) j -> p c j", p=P))
         with nc.allow_non_contiguous_dma(reason="one factor a partition and output slice"):
             nc.sync.dma_start(gm_sb[:], gm.rearrange("(c p) o -> p (c o)", p=P))
@@ -122,16 +124,13 @@ def tile_list_two_headpicks_largest_stepgap_residual_kernel(
         picked_last = [sb.tile([P, HALF], F32, name="picked_last%d" % h) for h in range(2)]
         larger = sb.tile([P, PACK, J], F32, align_bytes=64, tag="larger_then_w")
         u2 = sb.tile([P, J, PACK], BF16, align_bytes=64, tag="u2_then_xt")
-        u2_pair = sb.tile([P, 2, J], BF16)
-        for t in range(2):
+        so_early = [so_first[:, 0, :], so_first[:, 1, :], so_third[:]]
+        for t in range(3):
             nc.scalar.activation(picked[:, t, :], xo_sb[t][:].indirect(offs2_sb[:]), COPY)
-        nc.vector.tensor_tensor(larger[:, 0:2, :], picked[:, 0:2, :], so_first[:], ALU.max)
-        for t in range(2):
-            nc.scalar.activation(u2_pair[:, t, :], larger[:, t, :], COPY, scale=fl_sb[:, t:t + 1])
-        nc.vector.tensor_copy(u2[:, :, 0:2], u2_pair[:].rearrange("p t j -> p j t"))
-        nc.scalar.activation(picked[:, 2, :], xo_sb[2][:].indirect(offs2_sb[:]), COPY)
-        nc.vector.tensor_tensor(larger[:, 2, :], picked[:, 2, :], so_third[:], ALU.max)
-        nc.vector.tensor_scalar(u2[:, :, 2], larger[:, 2, :], fl_sb[:, 2:3], None, ALU.mult)
+            nc.vector.tensor_tensor(larger[:, t, :], picked[:, t, :], so_early[t], ALU.max)
+            nc.vector.tensor_scalar(
+                u2[:, :, t], larger[:, t, :], fl_sb[:, t:t + 1], None, ALU.mult
+            )
         for h in range(2):
             nc.scalar.activation(
                 picked_last[h][:], xo_sb[3][:].indirect(offs2_sb[:, 8 * h:8 * (h + 1)]), COPY
@@ -205,7 +204,7 @@ def tile_list_two_headpicks_largest_stepgap_residual_kernel(
                 nc.tensor.matmul_mx(
                     out=p_ps[h][c][:],
                     lhsT=wb_sb[:, P * c:P * (c + 1)].bitcast(E4M3),
-                    lhsT_scale=scales[:, WB_COL + P * c:WB_COL + P * (c + 1)],
+                    lhsT_scale=wb_plane[:, P * c:P * (c + 1)],
                     rhs=hid_codes[:, halves[h]].bitcast(E5M2),
                     rhs_scale=hid_scales[:, halves[h]],
                     start=True,

@@ -40,7 +40,6 @@ def tile_list_two_headpicks_largest_stepgap_residual_kernel(
         wb_plane = sb.tile([P, N], U8, align_bytes=64)
         w_raw = sb.tile([P, 2 * R], U8, align_bytes=64)
         w2_raw = sb.tile([P, 2 * R], U8, align_bytes=64)
-        xt_sb = sb.tile([P, T], U32, align_bytes=64)
         xo_sb = [sb.tile([P, Z], F32, name="xo_sb%d" % t) for t in range(PACK)]
         so_first = sb.tile([P, 2, J], F32)
         so_third = sb.tile([P, J], F32)
@@ -57,17 +56,17 @@ def tile_list_two_headpicks_largest_stepgap_residual_kernel(
         nc.gpsimd.memset(w_scale_raw[:, :R].bitcast(I32), 0)
         nc.gpsimd.memset(zero[:], 0.0)
         nc.gpsimd.memset(wb_plane[:].bitcast(I32), 0)
-        nc.scalar.activation(q_sb[:, 0, :], zero[:], COPY)
 
         xo_planes = xo.rearrange("(p t) z -> p t z", t=PACK)
         so_planes = so.rearrange("(p t) j -> p t j", t=PACK)
         nc.sync.dma_start(offs_sb[:], offs)
         nc.sync.dma_start(offs2_sb[:], offs2)
         nc.sync.dma_start(xo_sb[0][:], xo_planes[:, 0, :])
-        nc.sync.dma_start(w2_raw[:].bitcast(I32), w2_words[0].bitcast(I32))
-        nc.sync.dma_start(xt_scale_raw[0:P:8, :].bitcast(I32), xt_scales[0].bitcast(I32))
-        nc.sync.dma_start(w_scale_raw[0:P:8, R:].bitcast(I32), w2_scales[0].bitcast(I32))
-        nc.sync.dma_start(w_scale_raw[0:P:8, :R].bitcast(I32), w_scales[0].bitcast(I32))
+        nc.scalar.dma_start(w2_raw[:].bitcast(I32), w2_words[0].bitcast(I32))
+        nc.scalar.dma_start(xt_scale_raw[0:P:8, :].bitcast(I32), xt_scales[0].bitcast(I32))
+        nc.scalar.dma_start(w_scale_raw[0:P:8, R:].bitcast(I32), w2_scales[0].bitcast(I32))
+        nc.scalar.dma_start(w_scale_raw[0:P:8, :R].bitcast(I32), w_scales[0].bitcast(I32))
+        nc.scalar.activation(q_sb[:, 0, :], zero[:], COPY)
         nc.sync.dma_start(so_first[:], so_planes[:, 0:2, :])
         nc.gpsimd.dma_start(fl_sb[:], fl.rearrange("(p t) o -> p (t o)", t=PACK))
         nc.sync.dma_start(xo_sb[1][:], xo_planes[:, 1, :])
@@ -75,12 +74,9 @@ def tile_list_two_headpicks_largest_stepgap_residual_kernel(
         nc.sync.dma_start(so_third[:], so_planes[:, 2, :])
         nc.sync.dma_start(xo_sb[3][:], xo_planes[:, 3, :])
         nc.sync.dma_start(so_last[:], so_planes[:, 3, :])
-        nc.sync.dma_start(
-            xt_sb[:].bitcast(I32), xt_words[0].rearrange("p n t -> p (n t)").bitcast(I32)
-        )
         nc.sync.dma_start(w_raw[:].bitcast(I32), w_words[0].bitcast(I32))
 
-        xt_scale_picked = sb.tile([P, J], U8, align_bytes=64)
+        xt_scale_picked = sb.tile([P, J], U8, align_bytes=64, tag="xt_scales_then_words")
         nc.vector.tensor_copy(xt_scale_picked[:], xt_scale_raw[:].indirect(offs_sb[:]))
         nc.vector.tensor_copy(
             scales[:, W_COL:XT_COL].rearrange("p (w t m) -> p w t m", w=2, t=PACK),
@@ -90,6 +86,10 @@ def tile_list_two_headpicks_largest_stepgap_residual_kernel(
         for r in range(1, 4):
             nc.sync.dma_start(scales[r:P:32, :].bitcast(I32), scales[8 * r:P:32, :].bitcast(I32))
 
+        xt_sb = sb.tile([P, T], U32, align_bytes=64, tag="xt_scales_then_words")
+        nc.sync.dma_start(
+            xt_sb[:].bitcast(I32), xt_words[0].rearrange("p n t -> p (n t)").bitcast(I32)
+        )
         nc.sync.dma_start(
             wb_sb[:].bitcast(I32), wb_words[0].rearrange("p n t -> p (n t)").bitcast(I32)
         )
@@ -190,7 +190,6 @@ def tile_list_two_headpicks_largest_stepgap_residual_kernel(
             )
         hid_codes = sb.tile([P, J], U32, align_bytes=64)
         hid_scales = sb.tile([P, J], U8, align_bytes=64)
-        out_rows = out.rearrange("(c p) j -> p c j", p=P)
         p_ps = [
             [ps.tile([P, HALF], F32, name="p_ps%d%d" % (h, c)) for c in range(2)] for h in range(2)
         ]
@@ -210,11 +209,11 @@ def tile_list_two_headpicks_largest_stepgap_residual_kernel(
                     start=True,
                     stop=True,
                 )
-        for h, queue in ((0, nc.sync), (1, nc.scalar)):
-            result = sb.tile([P, 2, HALF], F32, name="result%d" % h)
-            for c in range(2):
+        for h in range(2):
+            for c, queue in ((0, nc.sync), (1, nc.scalar)):
+                result = sb.tile([P, HALF], F32, name="result%d%d" % (h, c))
                 nc.vector.scalar_tensor_tensor(
-                    result[:, c, :], p_ps[h][c][:], gm_sb[:, c:c + 1], rs_sb[:, c, halves[h]],
+                    result[:], p_ps[h][c][:], gm_sb[:, c:c + 1], rs_sb[:, c, halves[h]],
                     ALU.mult, ALU.add,
                 )
-            queue.dma_start(out_rows[:, :, halves[h]], result[:])
+                queue.dma_start(out[P * c:P * (c + 1), halves[h]], result[:])

import concourse.mybir as mybir

K, T, J, R, F, Z, N = 512, 512, 256, 512, 512, 1024, 256
FLOPS = 2 * J * (K * R + F * R + R * N)

F32 = mybir.dt.float32
BF16 = mybir.dt.bfloat16
I32 = mybir.dt.int32
U32 = mybir.dt.uint32
U16 = mybir.dt.uint16
U8 = mybir.dt.uint8
E4M3 = mybir.dt.float8_e4m3fn_x4
E5M2 = mybir.dt.float8_e5m2_x4
E2M1 = mybir.dt.float4_e2m1fn_x4
ALU = mybir.AluOpType
COPY = mybir.ActivationFunctionType.Copy

P = 128
PACK = 4
HALF = J // 2
QUARTER = J // 4
W_COL, W2_COL, XT_COL = 0, R, 2 * R
SCALE_COLS = XT_COL + J


def tile_list_two_headpicks_largest_stepgap_residual_kernel(
    tc, xt_words, xt_scales, w_words, w_scales, xo, fl, so, w2_words, w2_scales,
    wb_words, wb_scales, rs, gm, offs, offs2, out,
):
    nc = tc.nc
    with (
        tc.tile_pool(name="sbuf", bufs=1) as sb,
        tc.psum_pool(name="psum", bufs=1) as ps,
    ):
        offs_sb = sb.tile([P, J // 16], U16)
        offs2_sb = sb.tile([P, J // 16], U16)
        xt_scale_raw = sb.tile([P, T], U8, align_bytes=64)
        w_scale_raw = sb.tile([P, 2 * R], U8, align_bytes=64)
        scales = sb.tile([P, SCALE_COLS], U8, align_bytes=64)
        wb_plane = sb.tile([P, N], U8, align_bytes=64)
        w_raw = sb.tile([P, 2 * R], U8, align_bytes=64)
        w2_raw = sb.tile([P, 2 * R], U8, align_bytes=64)
        xo_sb = [sb.tile([P, Z], F32, name="xo_sb%d" % t) for t in range(PACK)]
        so_first = sb.tile([P, 2, J], F32)
        so_third = sb.tile([P, J], F32)
        so_last = sb.tile([P, J], F32)
        fl_sb = sb.tile([P, PACK], F32)
        gm_sb = sb.tile([P, 2], F32)
        wb_sb = sb.tile([P, N], U32, align_bytes=64)
        rs_sb = sb.tile([P, 2, J], F32)
        q_sb = sb.tile([P, J + 1, PACK], F32)

        zero = sb.tile([P, PACK], F32)
        nc.vector.memset(xt_scale_raw[:].bitcast(I32), 0)
        nc.vector.memset(w_scale_raw[:, R:].bitcast(I32), 0)
        nc.gpsimd.memset(w_scale_raw[:, :R].bitcast(I32), 0)
        nc.gpsimd.memset(zero[:], 0.0)
        nc.gpsimd.memset(wb_plane[:].bitcast(I32), 0)

        xo_planes = xo.rearrange("(p t) z -> p t z", t=PACK)
        so_planes = so.rearrange("(p t) j -> p t j", t=PACK)
        nc.sync.dma_start(offs_sb[:], offs)
        nc.sync.dma_start(offs2_sb[:], offs2)
        nc.sync.dma_start(xo_sb[0][:], xo_planes[:, 0, :])
        nc.scalar.dma_start(w2_raw[:].bitcast(I32), w2_words[0].bitcast(I32))
        nc.scalar.dma_start(xt_scale_raw[0:P:8, :].bitcast(I32), xt_scales[0].bitcast(I32))
        nc.scalar.dma_start(w_scale_raw[0:P:8, R:].bitcast(I32), w2_scales[0].bitcast(I32))
        nc.scalar.dma_start(w_scale_raw[0:P:8, :R].bitcast(I32), w_scales[0].bitcast(I32))
        nc.scalar.activation(q_sb[:, 0, :], zero[:], COPY)
        nc.sync.dma_start(so_first[:], so_planes[:, 0:2, :])
        nc.gpsimd.dma_start(fl_sb[:], fl.rearrange("(p t) o -> p (t o)", t=PACK))
        nc.sync.dma_start(xo_sb[1][:], xo_planes[:, 1, :])
        nc.sync.dma_start(xo_sb[2][:], xo_planes[:, 2, :])
        nc.sync.dma_start(so_third[:], so_planes[:, 2, :])
        nc.sync.dma_start(xo_sb[3][:], xo_planes[:, 3, :])
        nc.sync.dma_start(so_last[:], so_planes[:, 3, :])
        nc.sync.dma_start(w_raw[:].bitcast(I32), w_words[0].bitcast(I32))

        xt_scale_picked = sb.tile([P, J], U8, align_bytes=64, tag="xt_scales_then_words")
        nc.vector.tensor_copy(xt_scale_picked[:], xt_scale_raw[:].indirect(offs_sb[:]))
        nc.vector.tensor_copy(
            scales[:, W_COL:XT_COL].rearrange("p (w t m) -> p w t m", w=2, t=PACK),
            w_scale_raw[:].rearrange("p (w m t) -> p w t m", w=2, t=PACK),
        )
        nc.vector.tensor_copy(scales[:, XT_COL:].bitcast(I32), xt_scale_picked[:].bitcast(I32))
        for r in range(1, 4):
            nc.sync.dma_start(scales[r:P:32, :].bitcast(I32), scales[8 * r:P:32, :].bitcast(I32))

        xt_sb = sb.tile([P, T], U32, align_bytes=64, tag="xt_scales_then_words")
        nc.sync.dma_start(
            xt_sb[:].bitcast(I32), xt_words[0].rearrange("p n t -> p (n t)").bitcast(I32)
        )
        nc.sync.dma_start(
            wb_sb[:].bitcast(I32), wb_words[0].rearrange("p n t -> p (n t)").bitcast(I32)
        )
        for r in range(4):
            nc.sync.dma_start(wb_plane[r:P:32, :].bitcast(I32), wb_scales[0, r:16:4, :].bitcast(I32))
        nc.sync.dma_start(rs_sb[:], rs.rearrange("(c p) j -> p c j", p=P))
        with nc.allow_non_contiguous_dma(reason="one factor a partition and output slice"):
            nc.sync.dma_start(gm_sb[:], gm.rearrange("(c p) o -> p (c o)", p=P))

        def deal_words(dealt, raw):
            nc.vector.tensor_copy(
                dealt[:].bitcast(U16).rearrange("p (t m) -> p t m", t=PACK),
                raw[:].bitcast(U16).rearrange("p (m t) -> p t m", t=PACK),
            )

        w2_dealt = sb.tile([P, 2 * R], U8, align_bytes=64)
        deal_words(w2_dealt, w2_raw)

        def hidden_product(bank, dealt, w_col, codes, code_dtype, plane, h):
            for t in range(PACK):
                nc.tensor.matmul_mx(
                    out=bank[:, t, :],
                    lhsT=dealt[:, 2 * P * t:2 * P * (t + 1)].bitcast(E2M1),
                    lhsT_scale=scales[:, w_col + P * t:w_col + P * (t + 1)],
                    rhs=codes[:, h * HALF:(h + 1) * HALF].bitcast(code_dtype),
                    rhs_scale=plane[:, h * HALF:(h + 1) * HALF],
                    start=True,
                    stop=True,
                )

        picked = sb.tile([P, 3, J], F32)
        picked_last = [sb.tile([P, HALF], F32, name="picked_last%d" % h) for h in range(2)]
        larger = sb.tile([P, PACK, J], F32, align_bytes=64, tag="larger_then_w")
        u2 = sb.tile([P, J, PACK], BF16, align_bytes=64, tag="u2_then_xt")
        so_early = [so_first[:, 0, :], so_first[:, 1, :], so_third[:]]
        for t in range(3):
            nc.scalar.activation(picked[:, t, :], xo_sb[t][:].indirect(offs2_sb[:]), COPY)
            nc.vector.tensor_tensor(larger[:, t, :], picked[:, t, :], so_early[t], ALU.max)
            nc.vector.tensor_scalar(
                u2[:, :, t], larger[:, t, :], fl_sb[:, t:t + 1], None, ALU.mult
            )
        for h in range(2):
            nc.scalar.activation(
                picked_last[h][:], xo_sb[3][:].indirect(offs2_sb[:, 8 * h:8 * (h + 1)]), COPY
            )
        halves = [slice(h * HALF, (h + 1) * HALF) for h in range(2)]
        for h in range(2):
            nc.vector.tensor_tensor(
                larger[:, 3, halves[h]], picked_last[h][:], so_last[:, halves[h]], ALU.max
            )
        for h in range(2):
            nc.vector.tensor_scalar(
                u2[:, halves[h], 3], larger[:, 3, halves[h]], fl_sb[:, 3:4], None, ALU.mult
            )
        u2_codes = sb.tile([P, J], U32, align_bytes=64)
        u2_scales = sb.tile([P, J], U8, align_bytes=64)
        q_ps = [ps.tile([P, PACK, HALF], F32, name="q_ps%d" % h) for h in range(2)]
        for h in range(2):
            nc.vector.quantize_mx(
                out=u2_codes[:, halves[h]].bitcast(E4M3),
                scales=u2_scales[:, halves[h]],
                in_=u2[:, halves[h], :].rearrange("p j t -> p (j t)"),
            )
            hidden_product(q_ps[h], w2_dealt, W2_COL, u2_codes, E4M3, u2_scales, h)

        w_dealt = sb.tile([P, 2 * R], U8, align_bytes=64, tag="larger_then_w")
        deal_words(w_dealt, w_raw)
        xt_picked = sb.tile([P, J], U32, align_bytes=64, tag="u2_then_xt")
        nc.vector.tensor_copy(xt_picked[:], xt_sb[:].indirect(offs_sb[:]))
        a_ps = [ps.tile([P, PACK, HALF], F32, name="a_ps%d" % h) for h in range(2)]
        for h in range(2):
            hidden_product(a_ps[h], w_dealt, W_COL, xt_picked, E5M2, scales[:, XT_COL:], h)

        step = sb.tile([P, J, PACK], F32)
        for c in range(4):
            j0 = c * QUARTER
            in_bank = j0 % HALF
            nc.scalar.activation(
                q_sb[:, 1 + j0:1 + j0 + QUARTER, :],
                q_ps[c // 2][:, :, in_bank:in_bank + QUARTER].rearrange("p t j -> p j t"),
                COPY,
            )
            nc.vector.scalar_tensor_tensor(
                step[:, j0:j0 + QUARTER, :],
                q_sb[:, j0:j0 + QUARTER, :],
                -0.6,
                q_sb[:, 1 + j0:1 + j0 + QUARTER, :],
                ALU.mult,
                ALU.add,
            )
        hid = sb.tile([P, J, PACK], BF16, align_bytes=64)
        for h in range(2):
            nc.vector.tensor_tensor(
                hid[:, halves[h], :],
                step[:, halves[h], :],
                a_ps[h][:].rearrange("p t j -> p j t"),
                ALU.max,
            )
        hid_codes = sb.tile([P, J], U32, align_bytes=64)
        hid_scales = sb.tile([P, J], U8, align_bytes=64)
        p_ps = [
            [ps.tile([P, HALF], F32, name="p_ps%d%d" % (h, c)) for c in range(2)] for h in range(2)
        ]
        for h in range(2):
            nc.vector.quantize_mx(
                out=hid_codes[:, halves[h]].bitcast(E5M2),
                scales=hid_scales[:, halves[h]],
                in_=hid[:, halves[h], :].rearrange("p j t -> p (j t)"),
            )
            for c in range(2):
                nc.tensor.matmul_mx(
                    out=p_ps[h][c][:],
                    lhsT=wb_sb[:, P * c:P * (c + 1)].bitcast(E4M3),
                    lhsT_scale=wb_plane[:, P * c:P * (c + 1)],
                    rhs=hid_codes[:, halves[h]].bitcast(E5M2),
                    rhs_scale=hid_scales[:, halves[h]],
                    start=True,
                    stop=True,
                )
        for h in range(2):
            for c, queue in ((0, nc.sync), (1, nc.scalar)):
                result = sb.tile([P, HALF], F32, name="result%d%d" % (h, c))
                nc.vector.scalar_tensor_tensor(
                    result[:], p_ps[h][c][:], gm_sb[:, c:c + 1], rs_sb[:, c, halves[h]],
                    ALU.mult, ALU.add,
                )
                queue.dma_start(out[P * c:P * (c + 1), halves[h]], result[:])
